import numpy as np
import ml_dtypes


def mxq(x, axis, fmt="e4m3"):
    dtype, down = {"e4m3": (ml_dtypes.float8_e4m3fn, 7), "e5m2": (ml_dtypes.float8_e5m2, 14)}[fmt]
    v = np.moveaxis(np.asarray(x, np.float32).astype(ml_dtypes.bfloat16).astype(np.float64), axis, -1)
    blocks = v.reshape(v.shape[:-1] + (-1, 32))
    amax = np.abs(blocks).max(-1, keepdims=True)
    byte = np.maximum(np.where(amax > 0, np.frexp(amax)[1] - 1 + 127, 0) - down, 1)
    scale = np.exp2(byte - 127.0)
    codes = (blocks / scale).astype(np.float32).astype(dtype).astype(np.float64)
    return np.moveaxis((codes * scale).reshape(v.shape), -1, axis)


WIDE = False


def mx_kscale(k):
    if not WIDE:
        return np.ones(k)
    levels = np.array([10, -10, 5, -5, 0])
    if k % 512:
        return np.exp2(np.random.permutation(np.resize(levels, k // 32))).repeat(32)
    a = np.empty((k // 512, 16))
    for p in range(k // 512):
        a[p, :8] = np.random.permutation(np.resize(levels, 8))
        for g in range(8):
            far = levels[np.abs(levels - a[p, g]) >= 10]
            a[p, g + 8] = far[np.random.randint(len(far))]
    return np.exp2(a.ravel()).repeat(32)


def f64(x):
    return np.asarray(x).astype(np.float64)


def striped(idx):
    return np.tile(idx.reshape(-1, 16).T, (8, 1)).astype(np.uint16)


def unstriped(offs):
    return offs[:16].T.reshape(-1).astype(np.int64)


def striped8(idx):
    return np.concatenate([x.reshape(-1, 16).T for x in idx]).astype(np.uint16)


def runs(offs, k):
    lists = np.stack([offs[16 * r : 16 * r + 16].T.reshape(-1) for r in range(8)]).astype(np.int64)
    return lists[np.arange(k) % 512 // 64]


def pack_weight(w):
    k, n = w.shape
    w = f64(np.asarray(w, np.float32).astype(ml_dtypes.bfloat16)).reshape(k // 32, 32, n)
    amax = np.abs(w).max(1)
    byte = np.clip(np.where(amax > 0, np.frexp(amax)[1] - 1 + 127 - 7, 1), 1, 254)
    scaled = (w * np.exp2(127.0 - byte)[:, None, :]).reshape(k, n).astype(np.float32)
    words = np.ascontiguousarray(scaled.reshape(k // 512, 128, 4, n).transpose(0, 1, 3, 2)).astype(ml_dtypes.float8_e4m3fn).view(np.uint8)
    return words, np.ascontiguousarray(byte.astype(np.uint8).reshape(k // 512, 16, n))


def unpack_weight(words, scales):
    g, p, n, _ = words.shape
    vals = np.ascontiguousarray(words).view(ml_dtypes.float8_e4m3fn).astype(np.float64) * np.repeat(np.exp2(scales.astype(np.float64) - 127.0), 8, axis=1)[..., None]
    return vals.transpose(0, 1, 3, 2).reshape(g * 512, n)


K, T, S, V, N, H, U = 512, 2048, 1024, 512, 512, 512, 1024


def setup_inputs():
    n = np.random.standard_normal
    s = mx_kscale(K)[:, None]
    u = mx_kscale(H)
    packed_xT = pack_weight(n((K, T)) * s)
    return {
        "x_words": packed_xT[0],
        "x_scales": packed_xT[1],
        "w1": (n((K, H)) / np.sqrt(K) / s * u).astype(np.float32),
        "w2": (n((H, H)) / np.sqrt(H) / u[:, None] * u).astype(np.float32),
        "mem": (n((H, U)) * u[:, None]).astype(np.float32),
        "w3": (n((H, N)) / np.sqrt(H) / u[:, None]).astype(np.float32),
        "res": n((N, U)).astype(np.float32),
        "offs": striped(np.random.permutation(T)[:S]),
        "n1": striped8(np.stack([np.random.permutation(S) for _ in range(8)])),
        "n2": striped8(np.stack([np.random.permutation(U)[:V] for _ in range(8)])),
        "n3": striped8(np.stack([np.random.permutation(U) for _ in range(8)])),
    }


def reference(x_words, x_scales, w1, w2, mem, w3, res, offs, n1, n2, n3):
    xq = unpack_weight(x_words, x_scales)[:, unstriped(offs)]
    y = mxq(f64(w1), 0, "e4m3").T @ xq
    ln = y[np.arange(H)[:, None], runs(n1, H)]
    z = ln.reshape(H, V, 2).max(axis=2)
    h = mxq(f64(w2), 0, "e4m3").T @ mxq(z, 0, "e4m3")
    pg = f64(mem).copy()
    pg[np.arange(H)[:, None], runs(n2, H)] = h
    z2 = pg - (0.5 * (pg[np.arange(H)[:, None], runs(n3, H)]))
    return f64(res) + (mxq(f64(w3), 0, "e4m3").T @ mxq(z2, 0, "e4m3"))

@@ -1,0 +1,228 @@
+from contextlib import ExitStack
+
+import concourse.mybir as mybir
+
+K, T, S, V, N, H, U = 512, 2048, 1024, 512, 512, 512, 1024
+FLOPS = 2 * (K * H * S + H * H * V + H * N * U)
+
+F32 = mybir.dt.float32
+BF16 = mybir.dt.bfloat16
+I32 = mybir.dt.int32
+U32 = mybir.dt.uint32
+U16 = mybir.dt.uint16
+U8 = mybir.dt.uint8
+FP8X4 = mybir.dt.float8_e4m3fn_x4
+ALU = mybir.AluOpType
+COPY = mybir.ActivationFunctionType.Copy
+
+P = 128
+PACK = 4
+LANES = 16
+
+
+def tile_picked_deeppoolpagem_none_p_kernel(
+    tc, x_words, x_scales, w1, w2, mem, w3, res, offs, n1, n2, n3, out
+):
+    nc = tc.nc
+    with ExitStack() as ctx:
+        keep = ctx.enter_context(tc.tile_pool(name="keep", bufs=1))
+        psum = ctx.enter_context(tc.psum_pool(name="psum", bufs=1))
+
+        def sb(name, shape, dtype):
+            return keep.tile(shape, dtype, name=name, align_bytes=64)
+
+        def entries(list_tile, first, count):
+            return list_tile[:, first // LANES : (first + count) // LANES]
+
+        def quantize(codes, scales, values):
+            nc.vector.quantize_mx(out=codes.bitcast(FP8X4), scales=scales, in_=values)
+
+        def product(acc, lhs_codes, lhs_scales, rhs_codes, rhs_scales):
+            nc.tensor.matmul_mx(
+                out=acc, lhsT=lhs_codes.bitcast(FP8X4), lhsT_scale=lhs_scales,
+                rhs=rhs_codes.bitcast(FP8X4), rhs_scale=rhs_scales, start=True, stop=True,
+            )
+
+        offs_sb = keep.tile([P, S // LANES], U16, name="offs_sb")
+        n1_sb = keep.tile([P, S // LANES], U16, name="n1_sb")
+        n2_sb = keep.tile([P, V // LANES], U16, name="n2_sb")
+        n3_sb = keep.tile([P, U // LANES], U16, name="n3_sb")
+        table_scales = sb("table_scales", [P, T], U8)
+        table_words = sb("table_words", [P, T], U32)
+        nc.vector.memset(table_scales[:].bitcast(I32), 0)
+        nc.sync.dma_start(offs_sb[:], offs)
+        w1_rows = w1.rearrange("(p j) c -> p j c", j=PACK)
+        w1_raw = [sb("w1_raw%d" % u, [P, PACK, H // 2], F32) for u in range(2)]
+        nc.sync.dma_start(w1_raw[0][:], w1_rows[:, :, 0 : H // 2])
+        for q in range(4):
+            nc.sync.dma_start(table_scales[32 * q : 32 * q + 4, :].bitcast(I32), x_scales[0, 4 * q : 4 * q + 4, :].bitcast(I32))
+        nc.sync.dma_start(table_words[:].bitcast(I32), x_words[0].rearrange("p n t -> p (n t)").bitcast(I32))
+        nc.sync.dma_start(w1_raw[1][:], w1_rows[:, :, H // 2 : H])
+        nc.sync.dma_start(n1_sb[:], n1)
+        nc.sync.dma_start(n2_sb[:], n2)
+        mem_rows = mem.rearrange("(p t) w -> p t w", t=PACK)
+        page = [sb("page%d" % t, [P, U], F32) for t in range(PACK)]
+        for t in range(PACK):
+            nc.sync.dma_start(page[t][:], mem_rows[:, t, :])
+        w2_raw = sb("w2_raw", [P, PACK, H], F32)
+        nc.sync.dma_start(w2_raw[:], w2.rearrange("(p j) c -> p j c", j=PACK))
+        nc.sync.dma_start(n3_sb[:], n3)
+        w3_raw = sb("w3_raw", [P, PACK, N], F32)
+        nc.sync.dma_start(w3_raw[:], w3.rearrange("(p j) c -> p j c", j=PACK))
+        res_sb = sb("res_sb", [P, N // P, U], F32)
+        nc.sync.dma_start(res_sb[:], res.rearrange("(b p) w -> p b w", p=P))
+
+        banks = [psum.tile([P, 512], F32, name="bank%d" % b) for b in range(8)]
+
+        HALF = S // 2
+        pieces = [(0, 512), (512, 256), (768, 256)]
+        x_codes = [sb("x_codes%d" % u, [P, n], U32) for u, (first, n) in enumerate(pieces)]
+        x_bytes = sb("x_bytes", [P, S], U8)
+        w1_bf = sb("w1_bf", [P, PACK, P, PACK], BF16)
+        w1_codes = sb("w1_codes", [P, H], U32)
+        w1_scales = sb("w1_scales", [P, H], U8)
+
+        def deal(dst, raw, tiles):
+            nc.scalar.copy(
+                dst.rearrange("p t m j -> p m t j")[:, :, tiles, :], raw.rearrange("p j (m t) -> p m t j", t=PACK)[:, :, tiles, :]
+            )
+
+        def gather_words(u):
+            first, n = pieces[u]
+            nc.vector.tensor_copy(x_codes[u][:], table_words[:].indirect(entries(offs_sb, first, n)))
+
+        deal(w1_bf[:, :, 0 : P // 2, :], w1_raw[0][:], slice(0, PACK))
+        deal(w1_bf[:, :, P // 2 : P, :], w1_raw[1][:], slice(0, 1))
+        deal(w1_bf[:, :, P // 2 : P, :], w1_raw[1][:], slice(1, PACK))
+        nc.vector.tensor_copy(x_bytes[:], table_scales[:].indirect(offs_sb[:]))
+        w1_flat = w1_bf[:].rearrange("p t m j -> p (t m j)")
+        gather_words(0)
+        gather_words(1)
+        quantize(w1_codes[:, 0:P], w1_scales[:, 0:P], w1_flat[:, 0 : PACK * P])
+        gather_words(2)
+        quantize(w1_codes[:, P : 2 * P], w1_scales[:, P : 2 * P], w1_flat[:, PACK * P : 2 * PACK * P])
+        quantize(w1_codes[:, 2 * P :], w1_scales[:, 2 * P :], w1_flat[:, 2 * PACK * P :])
+        y = [sb("y%d" % t, [P, S], F32) for t in range(PACK)]
+        for t in range(PACK):
+            cols = slice(t * P, (t + 1) * P)
+            for u, (first, n) in enumerate(pieces):
+                acc = banks[(len(pieces) * t + u) % 8][:, 0:n]
+                product(acc, w1_codes[:, cols], w1_scales[:, cols], x_codes[u][:], x_bytes[:, first : first + n])
+                if t == 0 and u == 1:
+                    nc.vector.tensor_copy(y[t][:, first : first + n], acc)
+                else:
+                    nc.scalar.copy(y[t][:, first : first + n], acc)
+
+        w2_bf = sb("w2_bf", [P, PACK, P, PACK], BF16)
+        w2_codes = sb("w2_codes", [P, H], U32)
+        w2_scales = sb("w2_scales", [P, H], U8)
+        deal(w2_bf[:], w2_raw[:], slice(0, PACK))
+        w3_bf = sb("w3_bf", [P, N, PACK], BF16)
+        w3_codes = sb("w3_codes", [P, N], U32)
+        w3_scales = sb("w3_scales", [P, N], U8)
+
+        VH = V // 2
+        lined = [sb("lined%d" % u, [P, PACK, HALF], F32) for u in range(2)]
+        z_bf = [sb("z_bf%d" % u, [P, VH, PACK], BF16) for u in range(2)]
+        z_codes = [sb("z_codes%d" % u, [P, VH], U32) for u in range(2)]
+        z_scales = [sb("z_scales%d" % u, [P, VH], U8) for u in range(2)]
+        h = [sb("h%d" % u, [P, PACK, VH], F32) for u in range(2)]
+
+        def line_up(t, u):
+            nc.vector.tensor_copy(lined[u][:, t, :], y[t][:].indirect(entries(n1_sb, u * HALF, HALF)))
+
+        def pool_pairs(u):
+            pairs = lined[u][:].rearrange("p t (c i e) -> p c t i e", i=4, e=2)
+            nc.vector.tensor_tensor(
+                z_bf[u][:].rearrange("p (c i) t -> p c t i", i=4), pairs[:, :, :, :, 0], pairs[:, :, :, :, 1], ALU.max
+            )
+
+        def second_product(u):
+            quantize(z_codes[u][:], z_scales[u][:], z_bf[u][:].rearrange("p v t -> p (v t)"))
+            for t in range(PACK):
+                cols = slice(t * P, (t + 1) * P)
+                acc = banks[PACK * u + t][:, 0:VH]
+                product(acc, w2_codes[:, cols], w2_scales[:, cols], z_codes[u][:], z_scales[u][:])
+                nc.scalar.copy(h[u][:, t, :], acc)
+
+        for t in range(2):
+            for u in range(2):
+                line_up(t, u)
+        line_up(2, 0)
+        line_up(3, 0)
+        quantize(w2_codes[:], w2_scales[:], w2_bf[:].rearrange("p t m j -> p (t m j)"))
+        line_up(2, 1)
+        pool_pairs(0)
+        line_up(3, 1)
+        second_product(0)
+        pool_pairs(1)
+        nc.vector.tensor_copy(page[0][:].indirect(entries(n2_sb, 0, VH)), h[0][:, 0, :])
+        second_product(1)
+        nc.scalar.copy(w3_bf[:].rearrange("p (c i) j -> p c j i", i=4), w3_raw[:].rearrange("p j (c i) -> p c j i", i=4))
+
+        doubled = [sb("doubled%d" % t, [P, U], F32) for t in range(PACK)]
+        for t in range(1, PACK):
+            nc.vector.tensor_copy(page[t][:].indirect(entries(n2_sb, 0, VH)), h[0][:, t, :])
+        quantize(w3_codes[:], w3_scales[:], w3_bf[:].rearrange("p c j -> p (c j)"))
+        for t in range(PACK):
+            nc.vector.tensor_copy(page[t][:].indirect(entries(n2_sb, VH, VH)), h[1][:, t, :])
+            nc.scalar.activation(doubled[t][:], page[t][:], COPY, scale=2.0)
+
+        CH = 256
+        chunks = U // CH
+        last = chunks - 1
+        diff = [sb("diff%d" % c, [P, PACK, CH], F32) for c in range(chunks)]
+        out_rows = out.rearrange("(b p) w -> p b w", p=P)
+
+        def fetch(c, t):
+            cols = slice(c * CH, (c + 1) * CH)
+            nc.vector.tensor_tensor(diff[c][:, t, :], page[t][:].indirect(entries(n3_sb, c * CH, CH)), doubled[t][:, cols], ALU.subtract)
+
+        def round_z2(first, n, on_vector):
+            rounded = sb("z2_bf%d" % first, [P, n, PACK], BF16)
+            dst = rounded[:].rearrange("p (c i) t -> p c t i", i=4)
+            src = diff[first // CH][:, :, first % CH : first % CH + n].rearrange("p t (c i) -> p c t i", i=4)
+            if on_vector:
+                nc.vector.tensor_scalar(dst, src, -0.5, None, ALU.mult)
+            else:
+                nc.scalar.activation(dst, src, COPY, scale=-0.5)
+            return rounded
+
+        def third_product(first, n, rounded):
+            codes = sb("z2_codes%d" % first, [P, n], U32)
+            scales = sb("z2_scales%d" % first, [P, n], U8)
+            quantize(codes[:], scales[:], rounded[:].rearrange("p w t -> p (w t)"))
+            per_bank = 512 // n
+            for b in range(N // P):
+                cols = slice(b * P, (b + 1) * P)
+                acc = banks[first // P + b // per_bank][:, (b % per_bank) * n : (b % per_bank + 1) * n]
+                product(acc, w3_codes[:, cols], w3_scales[:, cols], codes[:], scales[:])
+
+        def add_residual(first, n, part):
+            per_bank = 512 // n
+            cols = slice(first, first + n)
+            blocks = slice(per_bank * part, per_bank * (part + 1))
+            result = sb("result%d" % (first // P + part), [P, per_bank, n], F32)
+            nc.vector.tensor_tensor(
+                result[:], banks[first // P + part][:].rearrange("p (b w) -> p b w", w=n), res_sb[:, blocks, cols], ALU.add
+            )
+            nc.sync.dma_start(out_rows[:, blocks, cols], result[:])
+
+        rounded = {}
+        for c in range(chunks):
+            for t in range(PACK):
+                if t == PACK - 1 and c >= 1:
+                    third_product((c - 1) * CH, CH, rounded[c - 1])
+                fetch(c, t)
+                if t < 2 and c >= 2:
+                    add_residual((c - 2) * CH, CH, t)
+            if c < last:
+                rounded[c] = round_z2(c * CH, CH, False)
+        tail_b = round_z2(last * CH + P, P, False)
+        add_residual((last - 1) * CH, CH, 0)
+        tail_a = round_z2(last * CH, P, True)
+        add_residual((last - 1) * CH, CH, 1)
+        third_product(last * CH, P, tail_a)
+        third_product(last * CH + P, P, tail_b)
+        add_residual(last * CH, P, 0)
+        add_residual(last * CH + P, P, 0)

@@ -1,6 +1,7 @@
 from contextlib import ExitStack
 
 import concourse.mybir as mybir
+from concourse.masks import make_identity
 
 K, T, S, V, N, H, U = 512, 2048, 1024, 512, 512, 512, 1024
 FLOPS = 2 * (K * H * S + H * H * V + H * N * U)
@@ -28,8 +29,8 @@ def tile_picked_deeppoolpagem_none_p_kernel(
         keep = ctx.enter_context(tc.tile_pool(name="keep", bufs=1))
         psum = ctx.enter_context(tc.psum_pool(name="psum", bufs=1))
 
-        def sb(name, shape, dtype):
-            return keep.tile(shape, dtype, name=name, align_bytes=64)
+        def sb(name, shape, dtype, tag=None, bufs=1):
+            return keep.tile(shape, dtype, name=name, tag=tag or name, bufs=bufs, align_bytes=64)
 
         def entries(list_tile, first, count):
             return list_tile[:, first // LANES : (first + count) // LANES]
@@ -76,34 +77,34 @@ def tile_picked_deeppoolpagem_none_p_kernel(
 
         HALF = S // 2
         pieces = [(0, 512), (512, 256), (768, 256)]
-        x_codes = [sb("x_codes%d" % u, [P, n], U32) for u, (first, n) in enumerate(pieces)]
+        x_codes = {}
         x_bytes = sb("x_bytes", [P, S], U8)
-        w1_bf = sb("w1_bf", [P, PACK, P, PACK], BF16)
+        w1_bf_first = sb("w1_bf_first", [P, 1, P, PACK], BF16, tag="first_then_last")
+        w1_bf_rest = sb("w1_bf_rest", [P, PACK - 1, P, PACK], BF16)
         w1_codes = sb("w1_codes", [P, H], U32)
         w1_scales = sb("w1_scales", [P, H], U8)
 
-        def deal(dst, raw, tiles):
-            nc.scalar.copy(
-                dst.rearrange("p t m j -> p m t j")[:, :, tiles, :], raw.rearrange("p j (m t) -> p m t j", t=PACK)[:, :, tiles, :]
-            )
+        def deal(copy, dst, raw, tiles):
+            copy(dst.rearrange("p t m j -> p m t j"), raw.rearrange("p j (m t) -> p m t j", t=PACK)[:, :, tiles, :])
 
-        def gather_words(u):
+        def gather_words(u, tag=None):
             first, n = pieces[u]
+            x_codes[u] = sb("x_codes%d" % u, [P, n], U32, tag=tag)
             nc.vector.tensor_copy(x_codes[u][:], table_words[:].indirect(entries(offs_sb, first, n)))
 
-        deal(w1_bf[:, :, 0 : P // 2, :], w1_raw[0][:], slice(0, PACK))
-        deal(w1_bf[:, :, P // 2 : P, :], w1_raw[1][:], slice(0, 1))
-        deal(w1_bf[:, :, P // 2 : P, :], w1_raw[1][:], slice(1, PACK))
+        deal(nc.scalar.copy, w1_bf_first[:, :, 0 : P // 2, :], w1_raw[0][:], slice(0, 1))
+        deal(nc.scalar.copy, w1_bf_rest[:, :, 0 : P // 2, :], w1_raw[0][:], slice(1, PACK))
+        deal(nc.scalar.copy, w1_bf_first[:, :, P // 2 : P, :], w1_raw[1][:], slice(0, 1))
         nc.vector.tensor_copy(x_bytes[:], table_scales[:].indirect(offs_sb[:]))
-        w1_flat = w1_bf[:].rearrange("p t m j -> p (t m j)")
         gather_words(0)
         gather_words(1)
-        quantize(w1_codes[:, 0:P], w1_scales[:, 0:P], w1_flat[:, 0 : PACK * P])
-        gather_words(2)
-        quantize(w1_codes[:, P : 2 * P], w1_scales[:, P : 2 * P], w1_flat[:, PACK * P : 2 * PACK * P])
-        quantize(w1_codes[:, 2 * P :], w1_scales[:, 2 * P :], w1_flat[:, 2 * PACK * P :])
+        quantize(w1_codes[:, 0:P], w1_scales[:, 0:P], w1_bf_first[:].rearrange("p t m j -> p (t m j)"))
+        gather_words(2, tag="first_then_last")
+        deal(nc.scalar.copy, w1_bf_rest[:, :, P // 2 : P, :], w1_raw[1][:], slice(1, PACK))
+        rest_flat = w1_bf_rest[:].rearrange("p t m j -> p (t m j)")
         y = [sb("y%d" % t, [P, S], F32) for t in range(PACK)]
-        for t in range(PACK):
+
+        def first_product(t):
             cols = slice(t * P, (t + 1) * P)
             for u, (first, n) in enumerate(pieces):
                 acc = banks[(len(pieces) * t + u) % 8][:, 0:n]
@@ -113,20 +114,28 @@ def tile_picked_deeppoolpagem_none_p_kernel(
                 else:
                     nc.scalar.copy(y[t][:, first : first + n], acc)
 
+        first_product(0)
+        quantize(w1_codes[:, P : 2 * P], w1_scales[:, P : 2 * P], rest_flat[:, 0 : PACK * P])
+        first_product(1)
+        quantize(w1_codes[:, 2 * P :], w1_scales[:, 2 * P :], rest_flat[:, PACK * P :])
+        first_product(2)
+        first_product(3)
+
         w2_bf = sb("w2_bf", [P, PACK, P, PACK], BF16)
         w2_codes = sb("w2_codes", [P, H], U32)
         w2_scales = sb("w2_scales", [P, H], U8)
-        deal(w2_bf[:], w2_raw[:], slice(0, PACK))
+        deal(nc.scalar.copy, w2_bf[:], w2_raw[:], slice(0, PACK))
         w3_bf = sb("w3_bf", [P, N, PACK], BF16)
         w3_codes = sb("w3_codes", [P, N], U32)
         w3_scales = sb("w3_scales", [P, N], U8)
+        nc.scalar.copy(w3_bf[:].rearrange("p (c i) j -> p c j i", i=4), w3_raw[:].rearrange("p j (c i) -> p c j i", i=4))
 
         VH = V // 2
-        lined = [sb("lined%d" % u, [P, PACK, HALF], F32) for u in range(2)]
+        lined = [sb("lined%d" % u, [P, PACK, HALF], BF16) for u in range(2)]
         z_bf = [sb("z_bf%d" % u, [P, VH, PACK], BF16) for u in range(2)]
         z_codes = [sb("z_codes%d" % u, [P, VH], U32) for u in range(2)]
         z_scales = [sb("z_scales%d" % u, [P, VH], U8) for u in range(2)]
-        h = [sb("h%d" % u, [P, PACK, VH], F32) for u in range(2)]
+        h = [sb("h%d" % t, [P, V], F32) for t in range(PACK)]
 
         def line_up(t, u):
             nc.vector.tensor_copy(lined[u][:, t, :], y[t][:].indirect(entries(n1_sb, u * HALF, HALF)))
@@ -143,7 +152,7 @@ def tile_picked_deeppoolpagem_none_p_kernel(
                 cols = slice(t * P, (t + 1) * P)
                 acc = banks[PACK * u + t][:, 0:VH]
                 product(acc, w2_codes[:, cols], w2_scales[:, cols], z_codes[u][:], z_scales[u][:])
-                nc.scalar.copy(h[u][:, t, :], acc)
+                nc.scalar.copy(h[t][:, u * VH : (u + 1) * VH], acc)
 
         for t in range(2):
             for u in range(2):
@@ -156,42 +165,67 @@ def tile_picked_deeppoolpagem_none_p_kernel(
         line_up(3, 1)
         second_product(0)
         pool_pairs(1)
-        nc.vector.tensor_copy(page[0][:].indirect(entries(n2_sb, 0, VH)), h[0][:, 0, :])
+        quantize(w3_codes[:], w3_scales[:], w3_bf[:].rearrange("p c j -> p (c j)"))
         second_product(1)
-        nc.scalar.copy(w3_bf[:].rearrange("p (c i) j -> p c j i", i=4), w3_raw[:].rearrange("p j (c i) -> p c j i", i=4))
 
         doubled = [sb("doubled%d" % t, [P, U], F32) for t in range(PACK)]
-        for t in range(1, PACK):
-            nc.vector.tensor_copy(page[t][:].indirect(entries(n2_sb, 0, VH)), h[0][:, t, :])
-        quantize(w3_codes[:], w3_scales[:], w3_bf[:].rearrange("p c j -> p (c j)"))
-        for t in range(PACK):
-            nc.vector.tensor_copy(page[t][:].indirect(entries(n2_sb, VH, VH)), h[1][:, t, :])
+        def put(t, first, n):
+            nc.vector.tensor_copy(page[t][:].indirect(entries(n2_sb, first, n)), h[t][:, first : first + n])
+
+        def double(t):
             nc.scalar.activation(doubled[t][:], page[t][:], COPY, scale=2.0)
+
+        TURNED = 2
+        identity = sb("identity", [P, P], F32)
+        make_identity(nc, identity[:])
+        res_turned = [sb("res_turned%d" % g, [P, N], F32) for g in range(TURNED)]
+        for g in range(TURNED):
+            for b in range(N // P):
+                nc.tensor.transpose(banks[4 + g][:, b * P : (b + 1) * P], res_sb[:, b, g * P : (g + 1) * P], identity[:])
+            nc.scalar.copy(res_turned[g][:], banks[4 + g][:])
+        put(0, 0, VH)
+        put(1, 0, V)
+        double(1)
+        put(0, VH, VH)
+        double(0)
+        for t in range(2, PACK):
+            put(t, 0, V)
+            double(t)
 
         CH = 256
         chunks = U // CH
         last = chunks - 1
-        diff = [sb("diff%d" % c, [P, PACK, CH], F32) for c in range(chunks)]
         out_rows = out.rearrange("(b p) w -> p b w", p=P)
+        work = {}
+
+        def open_chunk(c):
+            work[c] = sb("work%d" % c, [P, PACK * CH], F32, tag="work", bufs=2)
 
         def fetch(c, t):
             cols = slice(c * CH, (c + 1) * CH)
-            nc.vector.tensor_tensor(diff[c][:, t, :], page[t][:].indirect(entries(n3_sb, c * CH, CH)), doubled[t][:, cols], ALU.subtract)
+            nc.vector.tensor_tensor(
+                work[c][:, t * CH : (t + 1) * CH], page[t][:].indirect(entries(n3_sb, c * CH, CH)), doubled[t][:, cols], ALU.subtract
+            )
 
-        def round_z2(first, n, on_vector):
-            rounded = sb("z2_bf%d" % first, [P, n, PACK], BF16)
-            dst = rounded[:].rearrange("p (c i) t -> p c t i", i=4)
-            src = diff[first // CH][:, :, first % CH : first % CH + n].rearrange("p t (c i) -> p c t i", i=4)
-            if on_vector:
-                nc.vector.tensor_scalar(dst, src, -0.5, None, ALU.mult)
-            else:
-                nc.scalar.activation(dst, src, COPY, scale=-0.5)
+        def round_z2(rounded, first, n):
+            dst = rounded.rearrange("p (c i t) -> p c t i", i=4, t=PACK)
+            planes = work[first // CH][:, 0 : PACK * CH].rearrange("p (t w) -> p t w", t=PACK)
+            src = planes[:, :, first % CH : first % CH + n].rearrange("p t (c i) -> p c t i", i=4)
+            nc.scalar.activation(dst, src, COPY, scale=-0.5)
             return rounded
 
-        def third_product(first, n, rounded):
+        def round_chunk(c):
+            rounded = sb("z2_bf%d" % c, [P, PACK * CH], BF16)
+            return round_z2(rounded[:], c * CH, CH)
+
+        def quantize_z2(first, n, rounded):
             codes = sb("z2_codes%d" % first, [P, n], U32)
             scales = sb("z2_scales%d" % first, [P, n], U8)
-            quantize(codes[:], scales[:], rounded[:].rearrange("p w t -> p (w t)"))
+            quantize(codes[:], scales[:], rounded)
+            return codes, scales
+
+        def third_product(first, n, rounded):
+            codes, scales = quantize_z2(first, n, rounded)
             per_bank = 512 // n
             for b in range(N // P):
                 cols = slice(b * P, (b + 1) * P)
@@ -208,21 +242,62 @@ def tile_picked_deeppoolpagem_none_p_kernel(
             )
             nc.sync.dma_start(out_rows[:, blocks, cols], result[:])
 
-        rounded = {}
-        for c in range(chunks):
-            for t in range(PACK):
-                if t == PACK - 1 and c >= 1:
-                    third_product((c - 1) * CH, CH, rounded[c - 1])
-                fetch(c, t)
-                if t < 2 and c >= 2:
-                    add_residual((c - 2) * CH, CH, t)
-            if c < last:
-                rounded[c] = round_z2(c * CH, CH, False)
-        tail_b = round_z2(last * CH + P, P, False)
+        def turned_product(c, rounded):
+            codes, scales = quantize_z2(c * CH, CH, rounded)
+            for e in range(2):
+                cols = slice(e * P, (e + 1) * P)
+                product(banks[e][:], codes[:, cols], scales[:, cols], w3_codes[:], w3_scales[:])
+
+        def turn_back(c, e):
+            g = 2 * c + e
+            turned = sb("turned%d" % g, [P, N], F32)
+            nc.scalar.copy(turned[:], banks[e][:])
+            for b in range(N // P):
+                cols = slice(b * P, (b + 1) * P)
+                nc.tensor.matmul(banks[6 + e][:, cols], res_turned[g][:, cols], identity[:], start=True, stop=False, is_transpose=True)
+                nc.tensor.matmul(banks[6 + e][:, cols], turned[:, cols], identity[:], start=False, stop=True, is_transpose=True)
+
+        turned_result = [sb("result_turned%d" % c, [P, N // P, CH], F32) for c in range(1)]
+
+        def empty_turned(c, e):
+            nc.scalar.copy(turned_result[c][:, :, e * P : (e + 1) * P], banks[6 + e][:].rearrange("p (b w) -> p b w", w=P))
+
+        def store_turned(c):
+            nc.scalar.dma_start(out_rows[:, :, c * CH : (c + 1) * CH], turned_result[c][:])
+
+
+        open_chunk(0)
+        for t in range(PACK):
+            fetch(0, t)
+        rounded0 = round_chunk(0)
+        open_chunk(1)
+        for t in range(PACK):
+            fetch(1, t)
+        turned_product(0, rounded0)
+        rounded1 = round_chunk(1)
+        turn_back(0, 0)
+        turn_back(0, 1)
+        open_chunk(2)
+        for t in range(PACK):
+            fetch(2, t)
+        third_product(CH, CH, rounded1)
+        rounded2 = round_chunk(2)
+        empty_turned(0, 0)
+        empty_turned(0, 1)
+        store_turned(0)
+        open_chunk(3)
+        for t in range(PACK):
+            fetch(3, t)
+            if t in (1, 2):
+                add_residual(CH, CH, t - 1)
+        third_product(2 * CH, CH, rounded2)
+        tail_a = sb("tail_a", [P, PACK * P], BF16)
+        tail_b = sb("tail_b", [P, PACK * P], BF16)
+        round_z2(tail_a[:], last * CH, P)
+        round_z2(tail_b[:], last * CH + P, P)
+        third_product(last * CH, P, tail_a[:])
         add_residual((last - 1) * CH, CH, 0)
-        tail_a = round_z2(last * CH, P, True)
+        third_product(last * CH + P, P, tail_b[:])
         add_residual((last - 1) * CH, CH, 1)
-        third_product(last * CH, P, tail_a)
-        third_product(last * CH + P, P, tail_b)
         add_residual(last * CH, P, 0)
         add_residual(last * CH + P, P, 0)

from contextlib import ExitStack

import concourse.mybir as mybir
from concourse.masks import make_identity

K, T, S, V, N, H, U = 512, 2048, 1024, 512, 512, 512, 1024
FLOPS = 2 * (K * H * S + H * H * V + H * N * U)

F32 = mybir.dt.float32
BF16 = mybir.dt.bfloat16
I32 = mybir.dt.int32
U32 = mybir.dt.uint32
U16 = mybir.dt.uint16
U8 = mybir.dt.uint8
FP8X4 = mybir.dt.float8_e4m3fn_x4
ALU = mybir.AluOpType
COPY = mybir.ActivationFunctionType.Copy

P = 128
PACK = 4
LANES = 16


def tile_picked_deeppoolpagem_none_p_kernel(
    tc, x_words, x_scales, w1, w2, mem, w3, res, offs, n1, n2, n3, out
):
    nc = tc.nc
    with ExitStack() as ctx:
        keep = ctx.enter_context(tc.tile_pool(name="keep", bufs=1))
        psum = ctx.enter_context(tc.psum_pool(name="psum", bufs=1))

        def sb(name, shape, dtype, tag=None, bufs=1):
            return keep.tile(shape, dtype, name=name, tag=tag or name, bufs=bufs, align_bytes=64)

        def entries(list_tile, first, count):
            return list_tile[:, first // LANES : (first + count) // LANES]

        def quantize(codes, scales, values):
            nc.vector.quantize_mx(out=codes.bitcast(FP8X4), scales=scales, in_=values)

        def product(acc, lhs_codes, lhs_scales, rhs_codes, rhs_scales):
            nc.tensor.matmul_mx(
                out=acc, lhsT=lhs_codes.bitcast(FP8X4), lhsT_scale=lhs_scales,
                rhs=rhs_codes.bitcast(FP8X4), rhs_scale=rhs_scales, start=True, stop=True,
            )

        offs_sb = keep.tile([P, S // LANES], U16, name="offs_sb")
        n1_sb = keep.tile([P, S // LANES], U16, name="n1_sb")
        n2_sb = keep.tile([P, V // LANES], U16, name="n2_sb")
        n3_sb = keep.tile([P, U // LANES], U16, name="n3_sb")
        table_scales = sb("table_scales", [P, T], U8)
        table_words = sb("table_words", [P, T], U32)
        nc.vector.memset(table_scales[:].bitcast(I32), 0)
        nc.sync.dma_start(offs_sb[:], offs)
        w1_rows = w1.rearrange("(p j) c -> p j c", j=PACK)
        w1_raw = [sb("w1_raw%d" % u, [P, PACK, H // 2], F32) for u in range(2)]
        nc.sync.dma_start(w1_raw[0][:], w1_rows[:, :, 0 : H // 2])
        for q in range(4):
            nc.sync.dma_start(table_scales[32 * q : 32 * q + 4, :].bitcast(I32), x_scales[0, 4 * q : 4 * q + 4, :].bitcast(I32))
        nc.sync.dma_start(table_words[:].bitcast(I32), x_words[0].rearrange("p n t -> p (n t)").bitcast(I32))
        nc.sync.dma_start(w1_raw[1][:], w1_rows[:, :, H // 2 : H])
        nc.sync.dma_start(n1_sb[:], n1)
        nc.sync.dma_start(n2_sb[:], n2)
        mem_rows = mem.rearrange("(p t) w -> p t w", t=PACK)
        page = [sb("page%d" % t, [P, U], F32) for t in range(PACK)]
        for t in range(PACK):
            nc.sync.dma_start(page[t][:], mem_rows[:, t, :])
        w2_raw = sb("w2_raw", [P, PACK, H], F32)
        nc.sync.dma_start(w2_raw[:], w2.rearrange("(p j) c -> p j c", j=PACK))
        nc.sync.dma_start(n3_sb[:], n3)
        w3_raw = sb("w3_raw", [P, PACK, N], F32)
        nc.sync.dma_start(w3_raw[:], w3.rearrange("(p j) c -> p j c", j=PACK))
        res_sb = sb("res_sb", [P, N // P, U], F32)
        nc.sync.dma_start(res_sb[:], res.rearrange("(b p) w -> p b w", p=P))

        banks = [psum.tile([P, 512], F32, name="bank%d" % b) for b in range(8)]

        HALF = S // 2
        pieces = [(0, 512), (512, 256), (768, 256)]
        x_codes = {}
        x_bytes = sb("x_bytes", [P, S], U8)
        w1_bf_first = sb("w1_bf_first", [P, 1, P, PACK], BF16, tag="first_then_last")
        w1_bf_rest = sb("w1_bf_rest", [P, PACK - 1, P, PACK], BF16)
        w1_codes = sb("w1_codes", [P, H], U32)
        w1_scales = sb("w1_scales", [P, H], U8)

        def deal(copy, dst, raw, tiles):
            copy(dst.rearrange("p t m j -> p m t j"), raw.rearrange("p j (m t) -> p m t j", t=PACK)[:, :, tiles, :])

        def gather_words(u, tag=None):
            first, n = pieces[u]
            x_codes[u] = sb("x_codes%d" % u, [P, n], U32, tag=tag)
            nc.vector.tensor_copy(x_codes[u][:], table_words[:].indirect(entries(offs_sb, first, n)))

        deal(nc.scalar.copy, w1_bf_first[:, :, 0 : P // 2, :], w1_raw[0][:], slice(0, 1))
        deal(nc.scalar.copy, w1_bf_rest[:, :, 0 : P // 2, :], w1_raw[0][:], slice(1, PACK))
        deal(nc.scalar.copy, w1_bf_first[:, :, P // 2 : P, :], w1_raw[1][:], slice(0, 1))
        nc.vector.tensor_copy(x_bytes[:], table_scales[:].indirect(offs_sb[:]))
        gather_words(0)
        gather_words(1)
        quantize(w1_codes[:, 0:P], w1_scales[:, 0:P], w1_bf_first[:].rearrange("p t m j -> p (t m j)"))
        gather_words(2, tag="first_then_last")
        deal(nc.scalar.copy, w1_bf_rest[:, :, P // 2 : P, :], w1_raw[1][:], slice(1, PACK))
        rest_flat = w1_bf_rest[:].rearrange("p t m j -> p (t m j)")
        y = [sb("y%d" % t, [P, S], F32) for t in range(PACK)]

        def first_product(t):
            cols = slice(t * P, (t + 1) * P)
            for u, (first, n) in enumerate(pieces):
                acc = banks[(len(pieces) * t + u) % 8][:, 0:n]
                product(acc, w1_codes[:, cols], w1_scales[:, cols], x_codes[u][:], x_bytes[:, first : first + n])
                if t == 0 and u == 1:
                    nc.vector.tensor_copy(y[t][:, first : first + n], acc)
                else:
                    nc.scalar.copy(y[t][:, first : first + n], acc)

        first_product(0)
        quantize(w1_codes[:, P : 2 * P], w1_scales[:, P : 2 * P], rest_flat[:, 0 : PACK * P])
        first_product(1)
        quantize(w1_codes[:, 2 * P :], w1_scales[:, 2 * P :], rest_flat[:, PACK * P :])
        first_product(2)
        first_product(3)

        w2_bf = sb("w2_bf", [P, PACK, P, PACK], BF16)
        w2_codes = sb("w2_codes", [P, H], U32)
        w2_scales = sb("w2_scales", [P, H], U8)
        deal(nc.scalar.copy, w2_bf[:], w2_raw[:], slice(0, PACK))
        w3_bf = sb("w3_bf", [P, N, PACK], BF16)
        w3_codes = sb("w3_codes", [P, N], U32)
        w3_scales = sb("w3_scales", [P, N], U8)
        nc.scalar.copy(w3_bf[:].rearrange("p (c i) j -> p c j i", i=4), w3_raw[:].rearrange("p j (c i) -> p c j i", i=4))

        VH = V // 2
        lined = [sb("lined%d" % u, [P, PACK, HALF], BF16) for u in range(2)]
        z_bf = [sb("z_bf%d" % u, [P, VH, PACK], BF16) for u in range(2)]
        z_codes = [sb("z_codes%d" % u, [P, VH], U32) for u in range(2)]
        z_scales = [sb("z_scales%d" % u, [P, VH], U8) for u in range(2)]
        h = [sb("h%d" % t, [P, V], F32) for t in range(PACK)]

        def line_up(t, u):
            nc.vector.tensor_copy(lined[u][:, t, :], y[t][:].indirect(entries(n1_sb, u * HALF, HALF)))

        def pool_pairs(u):
            pairs = lined[u][:].rearrange("p t (c i e) -> p c t i e", i=4, e=2)
            nc.vector.tensor_tensor(
                z_bf[u][:].rearrange("p (c i) t -> p c t i", i=4), pairs[:, :, :, :, 0], pairs[:, :, :, :, 1], ALU.max
            )

        def second_product(u):
            quantize(z_codes[u][:], z_scales[u][:], z_bf[u][:].rearrange("p v t -> p (v t)"))
            for t in range(PACK):
                cols = slice(t * P, (t + 1) * P)
                acc = banks[PACK * u + t][:, 0:VH]
                product(acc, w2_codes[:, cols], w2_scales[:, cols], z_codes[u][:], z_scales[u][:])
                nc.scalar.copy(h[t][:, u * VH : (u + 1) * VH], acc)

        for t in range(2):
            for u in range(2):
                line_up(t, u)
        line_up(2, 0)
        line_up(3, 0)
        quantize(w2_codes[:], w2_scales[:], w2_bf[:].rearrange("p t m j -> p (t m j)"))
        line_up(2, 1)
        pool_pairs(0)
        line_up(3, 1)
        second_product(0)
        pool_pairs(1)
        quantize(w3_codes[:], w3_scales[:], w3_bf[:].rearrange("p c j -> p (c j)"))
        second_product(1)

        doubled = [sb("doubled%d" % t, [P, U], F32) for t in range(PACK)]
        def put(t, first, n):
            nc.vector.tensor_copy(page[t][:].indirect(entries(n2_sb, first, n)), h[t][:, first : first + n])

        def double(t):
            nc.scalar.activation(doubled[t][:], page[t][:], COPY, scale=2.0)

        TURNED = 2
        identity = sb("identity", [P, P], F32)
        make_identity(nc, identity[:])
        res_turned = [sb("res_turned%d" % g, [P, N], F32) for g in range(TURNED)]
        for g in range(TURNED):
            for b in range(N // P):
                nc.tensor.transpose(banks[4 + g][:, b * P : (b + 1) * P], res_sb[:, b, g * P : (g + 1) * P], identity[:])
            nc.scalar.copy(res_turned[g][:], banks[4 + g][:])
        put(0, 0, VH)
        put(1, 0, V)
        double(1)
        put(0, VH, VH)
        double(0)
        for t in range(2, PACK):
            put(t, 0, V)
            double(t)

        CH = 256
        chunks = U // CH
        last = chunks - 1
        out_rows = out.rearrange("(b p) w -> p b w", p=P)
        work = {}

        def open_chunk(c):
            work[c] = sb("work%d" % c, [P, PACK * CH], F32, tag="work", bufs=2)

        def fetch(c, t):
            cols = slice(c * CH, (c + 1) * CH)
            nc.vector.tensor_tensor(
                work[c][:, t * CH : (t + 1) * CH], page[t][:].indirect(entries(n3_sb, c * CH, CH)), doubled[t][:, cols], ALU.subtract
            )

        def round_z2(rounded, first, n):
            dst = rounded.rearrange("p (c i t) -> p c t i", i=4, t=PACK)
            planes = work[first // CH][:, 0 : PACK * CH].rearrange("p (t w) -> p t w", t=PACK)
            src = planes[:, :, first % CH : first % CH + n].rearrange("p t (c i) -> p c t i", i=4)
            nc.scalar.activation(dst, src, COPY, scale=-0.5)
            return rounded

        def round_chunk(c):
            rounded = sb("z2_bf%d" % c, [P, PACK * CH], BF16)
            return round_z2(rounded[:], c * CH, CH)

        def quantize_z2(first, n, rounded):
            codes = sb("z2_codes%d" % first, [P, n], U32)
            scales = sb("z2_scales%d" % first, [P, n], U8)
            quantize(codes[:], scales[:], rounded)
            return codes, scales

        def third_product(first, n, rounded):
            codes, scales = quantize_z2(first, n, rounded)
            per_bank = 512 // n
            for b in range(N // P):
                cols = slice(b * P, (b + 1) * P)
                acc = banks[first // P + b // per_bank][:, (b % per_bank) * n : (b % per_bank + 1) * n]
                product(acc, w3_codes[:, cols], w3_scales[:, cols], codes[:], scales[:])

        def add_residual(first, n, part):
            per_bank = 512 // n
            cols = slice(first, first + n)
            blocks = slice(per_bank * part, per_bank * (part + 1))
            result = sb("result%d" % (first // P + part), [P, per_bank, n], F32)
            nc.vector.tensor_tensor(
                result[:], banks[first // P + part][:].rearrange("p (b w) -> p b w", w=n), res_sb[:, blocks, cols], ALU.add
            )
            nc.sync.dma_start(out_rows[:, blocks, cols], result[:])

        def turned_product(c, rounded):
            codes, scales = quantize_z2(c * CH, CH, rounded)
            for e in range(2):
                cols = slice(e * P, (e + 1) * P)
                product(banks[e][:], codes[:, cols], scales[:, cols], w3_codes[:], w3_scales[:])

        def turn_back(c, e):
            g = 2 * c + e
            turned = sb("turned%d" % g, [P, N], F32)
            nc.scalar.copy(turned[:], banks[e][:])
            for b in range(N // P):
                cols = slice(b * P, (b + 1) * P)
                nc.tensor.matmul(banks[6 + e][:, cols], res_turned[g][:, cols], identity[:], start=True, stop=False, is_transpose=True)
                nc.tensor.matmul(banks[6 + e][:, cols], turned[:, cols], identity[:], start=False, stop=True, is_transpose=True)

        turned_result = [sb("result_turned%d" % c, [P, N // P, CH], F32) for c in range(1)]

        def empty_turned(c, e):
            nc.scalar.copy(turned_result[c][:, :, e * P : (e + 1) * P], banks[6 + e][:].rearrange("p (b w) -> p b w", w=P))

        def store_turned(c):
            nc.scalar.dma_start(out_rows[:, :, c * CH : (c + 1) * CH], turned_result[c][:])


        open_chunk(0)
        for t in range(PACK):
            fetch(0, t)
        rounded0 = round_chunk(0)
        open_chunk(1)
        for t in range(PACK):
            fetch(1, t)
        turned_product(0, rounded0)
        rounded1 = round_chunk(1)
        turn_back(0, 0)
        turn_back(0, 1)
        open_chunk(2)
        for t in range(PACK):
            fetch(2, t)
        third_product(CH, CH, rounded1)
        rounded2 = round_chunk(2)
        empty_turned(0, 0)
        empty_turned(0, 1)
        store_turned(0)
        open_chunk(3)
        for t in range(PACK):
            fetch(3, t)
            if t in (1, 2):
                add_residual(CH, CH, t - 1)
        third_product(2 * CH, CH, rounded2)
        tail_a = sb("tail_a", [P, PACK * P], BF16)
        tail_b = sb("tail_b", [P, PACK * P], BF16)
        round_z2(tail_a[:], last * CH, P)
        round_z2(tail_b[:], last * CH + P, P)
        third_product(last * CH, P, tail_a[:])
        add_residual((last - 1) * CH, CH, 0)
        third_product(last * CH + P, P, tail_b[:])
        add_residual((last - 1) * CH, CH, 1)
        add_residual(last * CH, P, 0)
        add_residual(last * CH + P, P, 0)
